import numpy as np
CORES = [7,15,23,39,47,63,71,79,87,95,119,127]
N = 12
R, W, T = 4096, 64, 256
CAPP = 64
def entries(a): return a.T.reshape(-1)
def pack(v, P): return np.ascontiguousarray(np.asarray(v, np.int32).reshape(-1, P).T)
def lists(rng, how):
    Q = rng.permutation(N * R)[:N * T]
    if how == "hotrank": Q = R * int(rng.integers(N)) + rng.permutation(R)[:N * T]
    if how == "own": Q = np.concatenate([R * r + rng.permutation(R)[:T] for r in range(N)])
    if how == "sorted": Q = np.sort(Q)
    if how == "edge":
        ends = np.concatenate([R * np.arange(N), R * np.arange(N) + R - 1]); rest = np.setdiff1d(rng.permutation(N * R), ends, assume_unique=True)
        Q = rng.permutation(np.concatenate([ends, rng.permutation(rest)[:N * T - 2 * N]]))
    if how in ("uniform", "full", "sorted", "edge"):
        O = np.stack([rng.permutation(np.repeat(rng.permutation(N)[:T // CAPP], CAPP)) if how == "full" else rng.permutation(np.repeat(np.arange(N), CAPP))[:T] for r in range(N)]).reshape(-1); Q = np.zeros(N * T, np.int64)
        for d in range(N):
            m = np.nonzero(O == d)[0]; w = rng.permutation(R)[:len(m)]
            if how == "edge" and len(m) >= 2: w[:2] = [0, R - 1]; w[2:] = 1 + rng.permutation(R - 2)[:len(m) - 2]
            Q[m] = R * d + w
        if how == "sorted": Q = np.sort(Q.reshape(N, T), axis=1).reshape(-1)
    return {"pos": np.stack([pack(q, 128) for q in Q.reshape(N, T)])}
def setup_inputs(rng):
    return dict({"tab": rng.standard_normal((N, R, W), dtype=np.float32), "new": rng.standard_normal((N, T, W), dtype=np.float32)}, **lists(rng, "uniform"))
def setup_inputs_edge(rng):
    d = setup_inputs(rng); d.update(lists(rng, "edge"))
    for k in ("tab", "new"): d[k] = (d[k].astype(np.float32) * 1048576.0).astype(d[k].dtype)
    return d
def setup_inputs_full(rng):
    d = setup_inputs(rng); d.update(lists(rng, "full"))
    for k in ("tab", "new"): d[k] = (d[k].astype(np.float32) * (1 / 1024.0)).astype(d[k].dtype)
    return d
def setup_inputs_sorted(rng):
    d = setup_inputs(rng); d.update(lists(rng, "sorted"))
    return d
def check_inputs(x):
    bad = []
    if x["pos"].min() < 0 or x["pos"].max() >= N * R: bad.append("pos out of range")
    if len(np.unique(x["pos"])) != x["pos"].size: bad.append("a place is named twice")
    if max(int(np.bincount(entries(a) // R, minlength=N).max()) for a in x["pos"]) > CAPP: bad.append("more than CAPP entries of a list point into one rank's part")
    return bad
def reference(tab, new, pos):
    A = np.concatenate(list(tab), axis=0)
    for r in range(N): A[entries(pos[r])] = new[r]
    return {"y": np.stack([A[R * r:R * r + R] for r in range(N)])}

@@ -1,0 +1,254 @@
+from concourse.bass import DstId, RemoteDMATransfer, IndirectOffsetOnAxis
+from concourse.mybir import AluOpType, AxisListType
+
+N = 12
+MW = 34
+L0 = 2
+
+SCRATCH = {
+    "posS": ("sbuf", [128, 2], "int32"),
+    "newS": ("sbuf", [128, 256], "float32"),
+    "win": ("sbuf", [128, 256], "float32"),
+    "val": ("sbuf", [128, 2], "float32"),
+    "tabD": ("sbuf", [128, 12], "float32"),
+    "rowi": ("sbuf", [128, 128], "float32"),
+    "ident": ("sbuf", [128, 128], "float32"),
+    "tri": ("sbuf", [128, 128], "bfloat16"),
+    "onesb": ("sbuf", [128, 128], "bfloat16"),
+    "tabInv": ("sbuf", [128, 256], "bfloat16"),
+    "tabX0": ("sbuf", [128, 256], "bfloat16"),
+    "tabX1": ("sbuf", [128, 256], "bfloat16"),
+    "tabIdx": ("sbuf", [128, 256], "bfloat16"),
+    "intT": ("sbuf", [128, 8], "int32"),
+    "colF": ("sbuf", [128, 8], "float32"),
+    "lo64": ("sbuf", [128, 2], "float32"),
+    "D": ("sbuf", [128, 24], "bfloat16"),
+    "rhsInv": ("sbuf", [128, 24], "bfloat16"),
+    "rhsHi": ("sbuf", [128, 24], "bfloat16"),
+    "rhsLo": ("sbuf", [128, 24], "bfloat16"),
+    "prod": ("sbuf", [128, 24], "float32"),
+    "rank": ("sbuf", [128, 2], "float32"),
+    "Einv": ("sbuf", [128, 512], "bfloat16"),
+    "Eidx": ("sbuf", [128, 512], "bfloat16"),
+    "off": ("sbuf", [128, 24], "uint16"),
+    "S": ("sbuf", [128, N * MW], "float32"),
+    "land": ("sbuf", [128, L0 + N * MW], "float32"),
+    "Cbuf": ("sbuf", [128, 384], "float32"),
+    "tile": ("sbuf", [128, 384], "float32"),
+    "idxF": ("sbuf", [128, 6], "float32"),
+    "idxI": ("sbuf", [128, 6], "int32"),
+    "psW": ("psum", [128, 512], "float32"),
+    "psC": ("psum", [128, 512], "float32"),
+    "psO": ("psum", [128, 512], "float32"),
+    "psX": ("psum", [128, 512], "float32"),
+    "psT0": ("psum", [128, 512], "float32"),
+    "psT1": ("psum", [128, 512], "float32"),
+    "psT2": ("psum", [128, 512], "float32"),
+}
+NEV = 60
+SEMAPHORES = ["arr0", "arr1", "arr2", "sent", "scat"] + ["e%d" % i for i in range(NEV)]
+
+
+def rank_program(g, core, T, topo):
+    s = T.rank_of(core)
+    if s is None:
+        return
+    V, A, P, SY = g.vector, g.scalar, g.tensor, g.sync
+    OP = AluOpType
+    used = [0]
+
+    def ev():
+        e = {"s": T.sem["e%d" % used[0]], "n": 0}
+        used[0] += 1
+        return e
+
+    def mark(ins, e, k=1):
+        ins.then_inc(e["s"], k)
+        e["n"] += k
+
+    def wait(q, *es):
+        for e in es:
+            q.wait_ge(e["s"], e["n"])
+
+    e_pos, e_new0, e_new1, e_tab = ev(), ev(), ev(), ev()
+    mark(SY.dma_start(T.posS[:], T.pos[:]), e_pos, 16)
+    mark(SY.dma_start(T.newS[:, 0:64], T.new[0:128, :]), e_new0, 16)
+    mark(A.dma_start(T.newS[:, 64:128], T.new[0:128, :]), e_new0, 16)
+    mark(SY.dma_start(T.newS[:, 128:192], T.new[128:256, :]), e_new1, 16)
+    mark(A.dma_start(T.newS[:, 192:256], T.new[128:256, :]), e_new1, 16)
+    mark(A.dma_start(T.y[:], T.tab[:]), e_tab, 16)
+
+    e_val, e_tabD, e_row, e_ti, e_tx = ev(), ev(), ev(), ev(), ev()
+    mark(g.iota(T.val[:], [[128, 2]], 0, 1, allow_small_or_imprecise_dtypes=True), e_val)
+    mark(g.iota(T.tabD[:, 0:s + 1], [[-1, s + 1]], s, 0, allow_small_or_imprecise_dtypes=True), e_tabD)
+    if s < N - 1:
+        mark(g.iota(T.tabD[:, s + 1:N], [[-1, N - 1 - s]], N - 1, 0, allow_small_or_imprecise_dtypes=True), e_tabD)
+    mark(g.iota(T.rowi[:], [[1, 128]], 0, 0, allow_small_or_imprecise_dtypes=True), e_row)
+    mark(g.iota(T.tabInv[:, 0:128], [[32, 2], [0, 4], [1, 16]], 0, 0, allow_small_or_imprecise_dtypes=True), e_ti)
+    mark(g.iota(T.tabX0[:], [[32, 2], [-64, 4], [1, 32]], 64 * (s % 4), 0, allow_small_or_imprecise_dtypes=True), e_tx)
+
+    e_ones, e_id, e_tri, e_ti2, e_x1, e_tix = ev(), ev(), ev(), ev(), ev(), ev()
+    mark(V.memset(T.onesb[:], 1.0), e_ones)
+    wait(V, e_val, e_row)
+    mark(V.tensor_scalar(T.ident[:], T.rowi[:], T.val[:, 0:1], None, OP.is_equal), e_id)
+    mark(V.tensor_scalar(T.tri[:], T.rowi[:], T.val[:, 0:1], None, OP.is_gt), e_tri)
+    wait(V, e_ti)
+    mark(V.tensor_scalar(T.tabInv[:, 128:256], T.tabInv[:, 0:128], 16.0, None, OP.add), e_ti2)
+    wait(V, e_tx)
+    mark(V.tensor_scalar(T.tabX1[:], T.tabX0[:], 0.0, 256.0, OP.is_lt, OP.mult), e_x1)
+    wait(V, e_x1)
+    mark(V.tensor_tensor(T.tabIdx[:], T.tabX0[:], T.tabX1[:], OP.add), e_tix)
+
+    e_d, e_df, e_D, e_b, e_cf, e_l64 = ev(), ev(), ev(), ev(), ev(), ev()
+    wait(V, e_pos)
+    mark(V.tensor_scalar(T.intT[:, 0:2], T.posS[:], 12, None, OP.arith_shift_right), e_d)
+    wait(V, e_d)
+    mark(V.tensor_copy(T.colF[:, 0:2], T.intT[:, 0:2]), e_df)
+    wait(V, e_df, e_tabD)
+    for c in range(2):
+        mark(V.tensor_scalar(T.D[:, 12 * c:12 * c + 12], T.tabD[:], T.colF[:, c:c + 1], None, OP.is_equal), e_D)
+
+    e_pw, e_pc = ev(), ev()
+    wait(P, e_new0, e_id)
+    mark(P.transpose(T.psW[:, 0:128], T.newS[:, 0:128], T.ident[:]), e_pw)
+    wait(P, e_D, e_tri, e_ones)
+    mark(P.matmul(T.psC[:, 0:12], T.tri[:], T.D[:, 0:12], True, True), e_pc)
+    mark(P.matmul(T.psC[:, 12:24], T.onesb[:], T.D[:, 0:12], True, False), e_pc)
+    mark(P.matmul(T.psC[:, 12:24], T.tri[:], T.D[:, 12:24], False, True), e_pc)
+    wait(P, e_new1)
+    mark(P.transpose(T.psW[:, 128:256], T.newS[:, 128:256], T.ident[:]), e_pw)
+
+    mark(V.tensor_scalar(T.intT[:, 2:4], T.posS[:], 63, None, OP.bitwise_and), e_b)
+    mark(V.tensor_scalar(T.intT[:, 4:6], T.posS[:], 0xFC0, None, OP.bitwise_and), e_b)
+    mark(V.tensor_scalar(T.intT[:, 6:8], T.posS[:], 6, 192, OP.logical_shift_right, OP.bitwise_and), e_b)
+    wait(V, e_b)
+    mark(V.tensor_copy(T.colF[:, 2:8], T.intT[:, 2:8]), e_cf)
+    wait(V, e_cf)
+    mark(V.tensor_scalar(T.lo64[:], T.colF[:, 2:4], 64.0, None, OP.add), e_l64)
+
+    from_copy = _copy_func()
+    e_ri, e_rx = ev(), ev()
+    wait(A, e_D, e_val)
+    for c in range(2):
+        mark(A.activation(T.rhsInv[:, 12 * c:12 * c + 12], T.D[:, 12 * c:12 * c + 12], from_copy,
+                          scale=T.val[:, c:c + 1]), e_ri)
+    wait(A, e_cf, e_l64)
+    for c in range(2):
+        mark(A.activation(T.rhsHi[:, 12 * c:12 * c + 12], T.D[:, 12 * c:12 * c + 12], from_copy,
+                          scale=T.colF[:, 4 + c:5 + c]), e_rx)
+        mark(A.activation(T.rhsLo[:, 12 * c:12 * c + 12], T.D[:, 12 * c:12 * c + 12], from_copy,
+                          scale=T.lo64[:, c:c + 1]), e_rx)
+
+    e_pr, e_rk, e_Ei, e_Ex, e_win = ev(), ev(), ev(), ev(), ev()
+    wait(V, e_pc, e_D)
+    mark(V.tensor_tensor(T.prod[:], T.psC[:, 0:24], T.D[:], OP.mult), e_pr)
+    wait(V, e_pr)
+    for c in range(2):
+        mark(V.tensor_reduce(T.rank[:, c:c + 1], T.prod[:, 12 * c:12 * c + 12], AxisListType.X, OP.add), e_rk)
+    wait(V, e_rk, e_ti2, e_tix)
+    for c in range(2):
+        mark(V.tensor_scalar(T.Einv[:, 256 * c:256 * c + 256], T.tabInv[:], T.rank[:, c:c + 1], None, OP.is_equal), e_Ei)
+    for c in range(2):
+        mark(V.tensor_scalar(T.Eidx[:, 256 * c:256 * c + 256], T.tabIdx[:], T.colF[:, 6 + c:7 + c],
+                             T.rank[:, c:c + 1], OP.subtract, OP.is_equal), e_Ex)
+    wait(V, e_pw)
+    mark(V.tensor_copy(T.win[:], T.psW[:, 0:256]), e_win)
+
+    e_po, e_px = ev(), ev()
+    wait(P, e_Ei, e_ri)
+    for B in range(2):
+        for c in range(2):
+            mark(P.matmul(T.psO[:, 12 * B:12 * B + 12], T.Einv[:, 256 * c + 128 * B:256 * c + 128 * B + 128],
+                          T.rhsInv[:, 12 * c:12 * c + 12], c == 0, c == 1), e_po)
+    wait(P, e_Ex, e_rx)
+    for H in range(2):
+        i = 0
+        for c in range(2):
+            for rh in (T.rhsHi, T.rhsLo):
+                mark(P.matmul(T.psX[:, 12 * H:12 * H + 12], T.Eidx[:, 256 * c + 128 * H:256 * c + 128 * H + 128],
+                              rh[:, 12 * c:12 * c + 12], i == 0, i == 3), e_px)
+                i += 1
+
+    e_off, e_lown = ev(), ev()
+    e_S = [ev(), ev(), ev()]
+    e_C = [ev(), ev(), ev()]
+    wait(V, e_po)
+    for B in range(2):
+        mark(V.tensor_copy(T.off[:, B:24:2], T.psO[:, 12 * B:12 * B + 12]), e_off)
+    wait(V, e_off, e_win)
+    for dl in range(N):
+        src = T.win[:, 0:256].indirect(T.off[:, 2 * dl:2 * dl + 2])
+        if dl == 0:
+            mark(V.tensor_copy(T.Cbuf[:, 0:32], src), e_C[0])
+        else:
+            mark(V.tensor_copy(T.S[:, MW * dl:MW * dl + 32], src), e_S[dl // 4])
+        if dl == 3:
+            wait(V, e_px)
+            for H in range(2):
+                mark(V.tensor_copy(T.S[:, MW + 32 + H:N * MW:MW], T.psX[:, 12 * H + 1:12 * H + 12]), e_S[0])
+            mark(V.tensor_copy(T.land[:, L0 + 32:L0 + 34], T.psX[:, 0:24:12]), e_lown)
+
+    sent = 0
+    for c in range(3):
+        dls = [dl for dl in range(4 * c, 4 * c + 4) if dl != 0]
+        dsts = [T.cores[(s - dl) % N] for dl in dls]
+        common = topo.mask(core, dsts[0])
+        for d in dsts:
+            if not topo.may_write(core, d):
+                raise ValueError("no direct way")
+            common &= topo.mask(core, d)
+        eng = [e for e in range(16) if (common >> e) & 1]
+        share = len(eng) // 4
+        sizes = [share] * len(dls)
+        if len(dls) == 3:
+            sizes[0] = 2 * share
+        trs = []
+        at = 0
+        for dl, d, n in zip(dls, dsts, sizes):
+            m = 0
+            for e in eng[at:at + n]:
+                m |= 1 << e
+            at += n
+            rid, pid, _se = topo.addr(d)
+            trs.append(RemoteDMATransfer(dst_ids=[DstId(rid=rid, pnc=pid)], dma_engine_mask=m,
+                                         remote_sem=T.sem["arr%d" % c],
+                                         src=T.S[:, MW * dl:MW * dl + MW],
+                                         dst=T.land[:, L0 + MW * dl:L0 + MW * dl + MW]))
+            sent += n
+        wait(g, e_S[c])
+        g.remote_dma_fused(trs, local_sem=T.sem.sent)
+    arrive = sent // 3
+
+    psT = [T.psT0, T.psT1, T.psT2]
+    wait(g, e_tab)
+    for c in range(3):
+        e_r, e_I, e_pt, e_t = ev(), ev(), ev(), ev()
+        V.wait_ge(T.sem["arr%d" % c], arrive)
+        for q in range(4):
+            dl = 4 * c + q
+            if dl:
+                mark(V.tensor_copy(T.Cbuf[:, 32 * dl:32 * dl + 32], T.land[:, L0 + MW * dl:L0 + MW * dl + 32]), e_C[c])
+        wait(P, e_C[c])
+        mark(P.transpose(psT[c][:, 0:128], T.Cbuf[:, 128 * c:128 * c + 128], T.ident[:]), e_pt)
+        if c == 0:
+            wait(V, e_lown)
+        for H in range(2):
+            a = L0 + 4 * MW * c + 32 + H
+            mark(V.tensor_reduce(T.idxF[:, 2 * c + H:2 * c + H + 1], T.land[:, a:a + 3 * MW + 1:MW],
+                                 AxisListType.X, OP.add), e_r)
+        wait(V, e_r)
+        mark(V.tensor_scalar(T.idxI[:, 2 * c:2 * c + 2], T.idxF[:, 2 * c:2 * c + 2], -64.0, None, OP.add), e_I)
+        wait(V, e_pt)
+        mark(V.tensor_copy(T.tile[:, 128 * c:128 * c + 128], psT[c][:, 0:128]), e_t)
+        wait(g, e_I, e_t)
+        for H in range(2):
+            g.indirect_dma_start(T.y[:], IndirectOffsetOnAxis(ap=T.idxI[:, 2 * c + H:2 * c + H + 1], axis=0),
+                                 T.tile[:, 128 * c + 64 * H:128 * c + 64 * H + 64], None,
+                                 bounds_check=4095, oob_is_err=False).then_inc(T.sem.scat, 16)
+    g.wait_ge(T.sem.scat, 96)
+    g.wait_ge(T.sem.sent, sent)
+
+
+def _copy_func():
+    from concourse.mybir import ActivationFunctionType
+    return ActivationFunctionType.Copy

@@ -1,7 +1,9 @@
 from concourse.bass import DstId, RemoteDMATransfer, IndirectOffsetOnAxis
-from concourse.mybir import AluOpType, AxisListType
+from concourse.mybir import AluOpType, AxisListType, ActivationFunctionType
 
 N = 12
+R = 4096
+GROWS = 128
 MW = 34
 L0 = 2
 
@@ -15,13 +17,14 @@ SCRATCH = {
     "ident": ("sbuf", [128, 128], "float32"),
     "tri": ("sbuf", [128, 128], "bfloat16"),
     "onesb": ("sbuf", [128, 128], "bfloat16"),
-    "tabInv": ("sbuf", [128, 256], "bfloat16"),
-    "tabX0": ("sbuf", [128, 256], "bfloat16"),
-    "tabX1": ("sbuf", [128, 256], "bfloat16"),
-    "tabIdx": ("sbuf", [128, 256], "bfloat16"),
+    "tabInv": ("sbuf", [128, 128], "bfloat16"),
+    "tabX0": ("sbuf", [128, 128], "bfloat16"),
+    "tabX1": ("sbuf", [128, 128], "bfloat16"),
+    "tabIdx": ("sbuf", [128, 128], "bfloat16"),
     "intT": ("sbuf", [128, 8], "int32"),
     "colF": ("sbuf", [128, 8], "float32"),
     "lo64": ("sbuf", [128, 2], "float32"),
+    "a32": ("sbuf", [128, 2], "float32"),
     "D": ("sbuf", [128, 24], "bfloat16"),
     "rhsInv": ("sbuf", [128, 24], "bfloat16"),
     "rhsHi": ("sbuf", [128, 24], "bfloat16"),
@@ -37,16 +40,17 @@ SCRATCH = {
     "tile": ("sbuf", [128, 384], "float32"),
     "idxF": ("sbuf", [128, 6], "float32"),
     "idxI": ("sbuf", [128, 6], "int32"),
-    "psW": ("psum", [128, 512], "float32"),
+    "psW0": ("psum", [128, 512], "float32"),
+    "psW1": ("psum", [128, 512], "float32"),
     "psC": ("psum", [128, 512], "float32"),
     "psO": ("psum", [128, 512], "float32"),
     "psX": ("psum", [128, 512], "float32"),
-    "psT0": ("psum", [128, 512], "float32"),
+    "psTa": ("psum", [128, 512], "float32"),
+    "psTb": ("psum", [128, 512], "float32"),
     "psT1": ("psum", [128, 512], "float32"),
-    "psT2": ("psum", [128, 512], "float32"),
 }
-NEV = 60
-SEMAPHORES = ["arr0", "arr1", "arr2", "sent", "scat"] + ["e%d" % i for i in range(NEV)]
+NEV = 64
+SEMAPHORES = ["arr0", "arr1", "arr2", "sent", "scat", "gtab"] + ["e%d" % i for i in range(NEV)]
 
 
 def rank_program(g, core, T, topo):
@@ -55,6 +59,7 @@ def rank_program(g, core, T, topo):
         return
     V, A, P, SY = g.vector, g.scalar, g.tensor, g.sync
     OP = AluOpType
+    COPY = ActivationFunctionType.Copy
     used = [0]
 
     def ev():
@@ -70,34 +75,36 @@ def rank_program(g, core, T, topo):
         for e in es:
             q.wait_ge(e["s"], e["n"])
 
+    def iota(out, pattern, base, cm, e):
+        mark(g.iota(out, pattern, base, cm, allow_small_or_imprecise_dtypes=True), e)
+
     e_pos, e_new0, e_new1, e_tab = ev(), ev(), ev(), ev()
     mark(SY.dma_start(T.posS[:], T.pos[:]), e_pos, 16)
     mark(SY.dma_start(T.newS[:, 0:64], T.new[0:128, :]), e_new0, 16)
     mark(A.dma_start(T.newS[:, 64:128], T.new[0:128, :]), e_new0, 16)
     mark(SY.dma_start(T.newS[:, 128:192], T.new[128:256, :]), e_new1, 16)
     mark(A.dma_start(T.newS[:, 192:256], T.new[128:256, :]), e_new1, 16)
-    mark(A.dma_start(T.y[:], T.tab[:]), e_tab, 16)
+    mark(A.dma_start(T.y[0:R - GROWS, :], T.tab[0:R - GROWS, :]), e_tab, 16)
 
     e_val, e_tabD, e_row, e_ti, e_tx = ev(), ev(), ev(), ev(), ev()
-    mark(g.iota(T.val[:], [[128, 2]], 0, 1, allow_small_or_imprecise_dtypes=True), e_val)
-    mark(g.iota(T.tabD[:, 0:s + 1], [[-1, s + 1]], s, 0, allow_small_or_imprecise_dtypes=True), e_tabD)
+    iota(T.val[:], [[128, 2]], 0, 1, e_val)
+    iota(T.tabD[:, 0:s + 1], [[-1, s + 1]], s, 0, e_tabD)
     if s < N - 1:
-        mark(g.iota(T.tabD[:, s + 1:N], [[-1, N - 1 - s]], N - 1, 0, allow_small_or_imprecise_dtypes=True), e_tabD)
-    mark(g.iota(T.rowi[:], [[1, 128]], 0, 0, allow_small_or_imprecise_dtypes=True), e_row)
-    mark(g.iota(T.tabInv[:, 0:128], [[32, 2], [0, 4], [1, 16]], 0, 0, allow_small_or_imprecise_dtypes=True), e_ti)
-    mark(g.iota(T.tabX0[:], [[32, 2], [-64, 4], [1, 32]], 64 * (s % 4), 0, allow_small_or_imprecise_dtypes=True), e_tx)
+        iota(T.tabD[:, s + 1:N], [[-1, N - 1 - s]], N - 1, 0, e_tabD)
+    iota(T.tabX0[:], [[-64, 4], [1, 32]], 64 * (s % 4), 0, e_tx)
+    iota(T.rowi[:], [[1, 128]], 0, 0, e_row)
+    iota(T.tabInv[:], [[32, 2], [0, 4], [1, 16]], 0, 0, e_ti)
+    g.dma_start(T.y[R - GROWS:R, :], T.tab[R - GROWS:R, :]).then_inc(T.sem.gtab, 16)
 
-    e_ones, e_id, e_tri, e_ti2, e_x1, e_tix = ev(), ev(), ev(), ev(), ev(), ev()
+    e_ones, e_id, e_tri, e_x1, e_tix = ev(), ev(), ev(), ev(), ev()
     mark(V.memset(T.onesb[:], 1.0), e_ones)
-    wait(V, e_val, e_row)
-    mark(V.tensor_scalar(T.ident[:], T.rowi[:], T.val[:, 0:1], None, OP.is_equal), e_id)
-    mark(V.tensor_scalar(T.tri[:], T.rowi[:], T.val[:, 0:1], None, OP.is_gt), e_tri)
-    wait(V, e_ti)
-    mark(V.tensor_scalar(T.tabInv[:, 128:256], T.tabInv[:, 0:128], 16.0, None, OP.add), e_ti2)
     wait(V, e_tx)
     mark(V.tensor_scalar(T.tabX1[:], T.tabX0[:], 0.0, 256.0, OP.is_lt, OP.mult), e_x1)
     wait(V, e_x1)
     mark(V.tensor_tensor(T.tabIdx[:], T.tabX0[:], T.tabX1[:], OP.add), e_tix)
+    wait(V, e_val, e_row)
+    mark(V.tensor_scalar(T.tri[:], T.rowi[:], T.val[:, 0:1], None, OP.is_gt), e_tri)
+    mark(V.tensor_scalar(T.ident[:], T.rowi[:], T.val[:, 0:1], None, OP.is_equal), e_id)
 
     e_d, e_df, e_D, e_b, e_cf, e_l64 = ev(), ev(), ev(), ev(), ev(), ev()
     wait(V, e_pos)
@@ -108,16 +115,17 @@ def rank_program(g, core, T, topo):
     for c in range(2):
         mark(V.tensor_scalar(T.D[:, 12 * c:12 * c + 12], T.tabD[:], T.colF[:, c:c + 1], None, OP.is_equal), e_D)
 
-    e_pw, e_pc = ev(), ev()
+    e_pw0, e_pw1, e_pc = ev(), ev(), ev()
     wait(P, e_new0, e_id)
-    mark(P.transpose(T.psW[:, 0:128], T.newS[:, 0:128], T.ident[:]), e_pw)
+    mark(P.transpose(T.psW0[:, 0:128], T.newS[:, 0:128], T.ident[:]), e_pw0)
     wait(P, e_D, e_tri, e_ones)
     mark(P.matmul(T.psC[:, 0:12], T.tri[:], T.D[:, 0:12], True, True), e_pc)
     mark(P.matmul(T.psC[:, 12:24], T.onesb[:], T.D[:, 0:12], True, False), e_pc)
     mark(P.matmul(T.psC[:, 12:24], T.tri[:], T.D[:, 12:24], False, True), e_pc)
     wait(P, e_new1)
-    mark(P.transpose(T.psW[:, 128:256], T.newS[:, 128:256], T.ident[:]), e_pw)
+    mark(P.transpose(T.psW1[:, 0:128], T.newS[:, 128:256], T.ident[:]), e_pw1)
 
+    e_win = ev()
     mark(V.tensor_scalar(T.intT[:, 2:4], T.posS[:], 63, None, OP.bitwise_and), e_b)
     mark(V.tensor_scalar(T.intT[:, 4:6], T.posS[:], 0xFC0, None, OP.bitwise_and), e_b)
     mark(V.tensor_scalar(T.intT[:, 6:8], T.posS[:], 6, 192, OP.logical_shift_right, OP.bitwise_and), e_b)
@@ -125,34 +133,42 @@ def rank_program(g, core, T, topo):
     mark(V.tensor_copy(T.colF[:, 2:8], T.intT[:, 2:8]), e_cf)
     wait(V, e_cf)
     mark(V.tensor_scalar(T.lo64[:], T.colF[:, 2:4], 64.0, None, OP.add), e_l64)
+    mark(V.tensor_scalar(T.a32[:], T.colF[:, 6:8], -32.0, None, OP.add), e_l64)
+    wait(V, e_pw0)
+    mark(V.tensor_copy(T.win[:, 0:128], T.psW0[:, 0:128]), e_win)
 
-    from_copy = _copy_func()
     e_ri, e_rx = ev(), ev()
     wait(A, e_D, e_val)
     for c in range(2):
-        mark(A.activation(T.rhsInv[:, 12 * c:12 * c + 12], T.D[:, 12 * c:12 * c + 12], from_copy,
+        mark(A.activation(T.rhsInv[:, 12 * c:12 * c + 12], T.D[:, 12 * c:12 * c + 12], COPY,
                           scale=T.val[:, c:c + 1]), e_ri)
     wait(A, e_cf, e_l64)
     for c in range(2):
-        mark(A.activation(T.rhsHi[:, 12 * c:12 * c + 12], T.D[:, 12 * c:12 * c + 12], from_copy,
+        mark(A.activation(T.rhsHi[:, 12 * c:12 * c + 12], T.D[:, 12 * c:12 * c + 12], COPY,
                           scale=T.colF[:, 4 + c:5 + c]), e_rx)
-        mark(A.activation(T.rhsLo[:, 12 * c:12 * c + 12], T.D[:, 12 * c:12 * c + 12], from_copy,
+        mark(A.activation(T.rhsLo[:, 12 * c:12 * c + 12], T.D[:, 12 * c:12 * c + 12], COPY,
                           scale=T.lo64[:, c:c + 1]), e_rx)
 
-    e_pr, e_rk, e_Ei, e_Ex, e_win = ev(), ev(), ev(), ev(), ev()
+    e_pr, e_rk, e_Ei, e_Ex = ev(), ev(), ev(), ev()
     wait(V, e_pc, e_D)
     mark(V.tensor_tensor(T.prod[:], T.psC[:, 0:24], T.D[:], OP.mult), e_pr)
     wait(V, e_pr)
     for c in range(2):
         mark(V.tensor_reduce(T.rank[:, c:c + 1], T.prod[:, 12 * c:12 * c + 12], AxisListType.X, OP.add), e_rk)
-    wait(V, e_rk, e_ti2, e_tix)
-    for c in range(2):
-        mark(V.tensor_scalar(T.Einv[:, 256 * c:256 * c + 256], T.tabInv[:], T.rank[:, c:c + 1], None, OP.is_equal), e_Ei)
-    for c in range(2):
-        mark(V.tensor_scalar(T.Eidx[:, 256 * c:256 * c + 256], T.tabIdx[:], T.colF[:, 6 + c:7 + c],
-                             T.rank[:, c:c + 1], OP.subtract, OP.is_equal), e_Ex)
-    wait(V, e_pw)
-    mark(V.tensor_copy(T.win[:], T.psW[:, 0:256]), e_win)
+    wait(V, e_rk, e_ti, e_tix, e_l64)
+    for B in range(2):
+        for c in range(2):
+            o = 256 * c + 128 * B
+            mark(V.tensor_scalar(T.Einv[:, o:o + 128], T.tabInv[:], 16.0 * B, T.rank[:, c:c + 1],
+                                 OP.add, OP.is_equal), e_Ei)
+    for H in range(2):
+        for c in range(2):
+            o = 256 * c + 128 * H
+            acol = T.colF[:, 6 + c:7 + c] if H == 0 else T.a32[:, c:c + 1]
+            mark(V.tensor_scalar(T.Eidx[:, o:o + 128], T.tabIdx[:], acol, T.rank[:, c:c + 1],
+                                 OP.subtract, OP.is_equal), e_Ex)
+    wait(V, e_pw1)
+    mark(V.tensor_copy(T.win[:, 128:256], T.psW1[:, 0:128]), e_win)
 
     e_po, e_px = ev(), ev()
     wait(P, e_Ei, e_ri)
@@ -176,16 +192,14 @@ def rank_program(g, core, T, topo):
     for B in range(2):
         mark(V.tensor_copy(T.off[:, B:24:2], T.psO[:, 12 * B:12 * B + 12]), e_off)
     wait(V, e_off, e_win)
-    for dl in range(N):
+    for dl in range(1, N):
         src = T.win[:, 0:256].indirect(T.off[:, 2 * dl:2 * dl + 2])
-        if dl == 0:
-            mark(V.tensor_copy(T.Cbuf[:, 0:32], src), e_C[0])
-        else:
-            mark(V.tensor_copy(T.S[:, MW * dl:MW * dl + 32], src), e_S[dl // 4])
+        mark(V.tensor_copy(T.S[:, MW * dl:MW * dl + 32], src), e_S[dl // 4])
         if dl == 3:
             wait(V, e_px)
             for H in range(2):
                 mark(V.tensor_copy(T.S[:, MW + 32 + H:N * MW:MW], T.psX[:, 12 * H + 1:12 * H + 12]), e_S[0])
+            mark(V.tensor_copy(T.Cbuf[:, 0:32], T.win[:, 0:256].indirect(T.off[:, 0:2])), e_C[0])
             mark(V.tensor_copy(T.land[:, L0 + 32:L0 + 34], T.psX[:, 0:24:12]), e_lown)
 
     sent = 0
@@ -219,36 +233,53 @@ def rank_program(g, core, T, topo):
         g.remote_dma_fused(trs, local_sem=T.sem.sent)
     arrive = sent // 3
 
-    psT = [T.psT0, T.psT1, T.psT2]
+    def scatter(c, H):
+        g.indirect_dma_start(T.y[:], IndirectOffsetOnAxis(ap=T.idxI[:, 2 * c + H:2 * c + H + 1], axis=0),
+                             T.tile[:, 128 * c + 64 * H:128 * c + 64 * H + 64], None,
+                             bounds_check=4095, oob_is_err=False).then_inc(T.sem.scat, 16)
+
     wait(g, e_tab)
+    g.wait_ge(T.sem.gtab, 16)
     for c in range(3):
-        e_r, e_I, e_pt, e_t = ev(), ev(), ev(), ev()
+        e_r, e_I = ev(), ev()
         V.wait_ge(T.sem["arr%d" % c], arrive)
         for q in range(4):
             dl = 4 * c + q
             if dl:
                 mark(V.tensor_copy(T.Cbuf[:, 32 * dl:32 * dl + 32], T.land[:, L0 + MW * dl:L0 + MW * dl + 32]), e_C[c])
         wait(P, e_C[c])
-        mark(P.transpose(psT[c][:, 0:128], T.Cbuf[:, 128 * c:128 * c + 128], T.ident[:]), e_pt)
         if c == 0:
+            e_pt = [ev(), ev()]
+            for H, ps in enumerate((T.psTa, T.psTb)):
+                mark(P.transpose(ps[:, 0:64], T.Cbuf[64 * H:64 * H + 64, 0:128],
+                                 T.ident[64 * H:64 * H + 64, 64 * H:64 * H + 64]), e_pt[H])
             wait(V, e_lown)
+        else:
+            e_pt = [ev()]
+            ps = T.psT1 if c == 1 else T.psW0
+            if c == 2:
+                wait(P, e_win)
+            mark(P.transpose(ps[:, 0:128], T.Cbuf[:, 128 * c:128 * c + 128], T.ident[:]), e_pt[0])
         for H in range(2):
             a = L0 + 4 * MW * c + 32 + H
             mark(V.tensor_reduce(T.idxF[:, 2 * c + H:2 * c + H + 1], T.land[:, a:a + 3 * MW + 1:MW],
                                  AxisListType.X, OP.add), e_r)
         wait(V, e_r)
         mark(V.tensor_scalar(T.idxI[:, 2 * c:2 * c + 2], T.idxF[:, 2 * c:2 * c + 2], -64.0, None, OP.add), e_I)
-        wait(V, e_pt)
-        mark(V.tensor_copy(T.tile[:, 128 * c:128 * c + 128], psT[c][:, 0:128]), e_t)
-        wait(g, e_I, e_t)
-        for H in range(2):
-            g.indirect_dma_start(T.y[:], IndirectOffsetOnAxis(ap=T.idxI[:, 2 * c + H:2 * c + H + 1], axis=0),
-                                 T.tile[:, 128 * c + 64 * H:128 * c + 64 * H + 64], None,
-                                 bounds_check=4095, oob_is_err=False).then_inc(T.sem.scat, 16)
+        wait(g, e_I)
+        if c == 0:
+            for H, ps in enumerate((T.psTa, T.psTb)):
+                e_t = ev()
+                wait(V, e_pt[H])
+                mark(V.tensor_copy(T.tile[:, 64 * H:64 * H + 64], ps[:, 0:64]), e_t)
+                wait(g, e_t)
+                scatter(c, H)
+        else:
+            e_t = ev()
+            wait(V, e_pt[0])
+            mark(V.tensor_copy(T.tile[:, 128 * c:128 * c + 128], ps[:, 0:128]), e_t)
+            wait(g, e_t)
+            scatter(c, 0)
+            scatter(c, 1)
     g.wait_ge(T.sem.scat, 96)
     g.wait_ge(T.sem.sent, sent)
-
-
-def _copy_func():
-    from concourse.mybir import ActivationFunctionType
-    return ActivationFunctionType.Copy

@@ -4,8 +4,8 @@ from concourse.mybir import AluOpType, AxisListType, ActivationFunctionType
 N = 12
 R = 4096
 GROWS = 128
-MW = 34
-L0 = 2
+MW = 33
+NS = 6
 
 SCRATCH = {
     "posS": ("sbuf", [128, 2], "int32"),
@@ -15,16 +15,14 @@ SCRATCH = {
     "tabD": ("sbuf", [128, 12], "float32"),
     "rowi": ("sbuf", [128, 128], "float32"),
     "ident": ("sbuf", [128, 128], "float32"),
+    "J": ("sbuf", [128, 64], "float32"),
     "tri": ("sbuf", [128, 128], "bfloat16"),
     "onesb": ("sbuf", [128, 128], "bfloat16"),
     "tabInv": ("sbuf", [128, 128], "bfloat16"),
-    "tabX0": ("sbuf", [128, 128], "bfloat16"),
-    "tabX1": ("sbuf", [128, 128], "bfloat16"),
     "tabIdx": ("sbuf", [128, 128], "bfloat16"),
     "intT": ("sbuf", [128, 8], "int32"),
     "colF": ("sbuf", [128, 8], "float32"),
     "lo64": ("sbuf", [128, 2], "float32"),
-    "a32": ("sbuf", [128, 2], "float32"),
     "D": ("sbuf", [128, 24], "bfloat16"),
     "rhsInv": ("sbuf", [128, 24], "bfloat16"),
     "rhsHi": ("sbuf", [128, 24], "bfloat16"),
@@ -32,14 +30,14 @@ SCRATCH = {
     "prod": ("sbuf", [128, 24], "float32"),
     "rank": ("sbuf", [128, 2], "float32"),
     "Einv": ("sbuf", [128, 512], "bfloat16"),
-    "Eidx": ("sbuf", [128, 512], "bfloat16"),
+    "Eidx": ("sbuf", [128, 256], "bfloat16"),
     "off": ("sbuf", [128, 24], "uint16"),
     "S": ("sbuf", [128, N * MW], "float32"),
-    "land": ("sbuf", [128, L0 + N * MW], "float32"),
-    "Cbuf": ("sbuf", [128, 384], "float32"),
-    "tile": ("sbuf", [128, 384], "float32"),
-    "idxF": ("sbuf", [128, 6], "float32"),
-    "idxI": ("sbuf", [128, 6], "int32"),
+    "land": ("sbuf", [128, N * MW], "float32"),
+    "ownX": ("sbuf", [128, 1], "float32"),
+    "Z": ("sbuf", [128, 128 * NS], "float32"),
+    "tile": ("sbuf", [128, 64 * NS], "float32"),
+    "idxI": ("sbuf", [128, NS], "int32"),
     "psW0": ("psum", [128, 512], "float32"),
     "psW1": ("psum", [128, 512], "float32"),
     "psC": ("psum", [128, 512], "float32"),
@@ -47,10 +45,10 @@ SCRATCH = {
     "psX": ("psum", [128, 512], "float32"),
     "psTa": ("psum", [128, 512], "float32"),
     "psTb": ("psum", [128, 512], "float32"),
-    "psT1": ("psum", [128, 512], "float32"),
+    "psTc": ("psum", [128, 512], "float32"),
 }
-NEV = 64
-SEMAPHORES = ["arr0", "arr1", "arr2", "sent", "scat", "gtab"] + ["e%d" % i for i in range(NEV)]
+NEV = 100
+SEMAPHORES = ["arr%d" % i for i in range(NS)] + ["sent", "scat", "gtab"] + ["e%d" % i for i in range(NEV)]
 
 
 def rank_program(g, core, T, topo):
@@ -86,22 +84,25 @@ def rank_program(g, core, T, topo):
     mark(A.dma_start(T.newS[:, 192:256], T.new[128:256, :]), e_new1, 16)
     mark(A.dma_start(T.y[0:R - GROWS, :], T.tab[0:R - GROWS, :]), e_tab, 16)
 
-    e_val, e_tabD, e_row, e_ti, e_tx = ev(), ev(), ev(), ev(), ev()
+    e_val, e_tabD, e_row, e_ti, e_tix = ev(), ev(), ev(), ev(), ev()
     iota(T.val[:], [[128, 2]], 0, 1, e_val)
     iota(T.tabD[:, 0:s + 1], [[-1, s + 1]], s, 0, e_tabD)
     if s < N - 1:
         iota(T.tabD[:, s + 1:N], [[-1, N - 1 - s]], N - 1, 0, e_tabD)
-    iota(T.tabX0[:], [[-64, 4], [1, 32]], 64 * (s % 4), 0, e_tx)
     iota(T.rowi[:], [[1, 128]], 0, 0, e_row)
     iota(T.tabInv[:], [[32, 2], [0, 4], [1, 16]], 0, 0, e_ti)
+    if s % 2 == 0:
+        iota(T.tabIdx[:], [[64, 2], [1, 64]], 0, 0, e_tix)
+    else:
+        iota(T.tabIdx[:], [[-64, 2], [1, 64]], 64, 0, e_tix)
     g.dma_start(T.y[R - GROWS:R, :], T.tab[R - GROWS:R, :]).then_inc(T.sem.gtab, 16)
 
-    e_ones, e_id, e_tri, e_x1, e_tix = ev(), ev(), ev(), ev(), ev()
+    e_ones, e_id, e_tri, e_z = ev(), ev(), ev(), ev()
     mark(V.memset(T.onesb[:], 1.0), e_ones)
-    wait(V, e_tx)
-    mark(V.tensor_scalar(T.tabX1[:], T.tabX0[:], 0.0, 256.0, OP.is_lt, OP.mult), e_x1)
-    wait(V, e_x1)
-    mark(V.tensor_tensor(T.tabIdx[:], T.tabX0[:], T.tabX1[:], OP.add), e_tix)
+    mark(V.memset(T.Z[:, 0:256], 0.0), e_z)
+    wait(A, e_row)
+    for j in range(2, NS):
+        mark(A.activation(T.Z[:, 128 * j:128 * j + 128], T.rowi[:], COPY, scale=0.0), e_z)
     wait(V, e_val, e_row)
     mark(V.tensor_scalar(T.tri[:], T.rowi[:], T.val[:, 0:1], None, OP.is_gt), e_tri)
     mark(V.tensor_scalar(T.ident[:], T.rowi[:], T.val[:, 0:1], None, OP.is_equal), e_id)
@@ -128,12 +129,11 @@ def rank_program(g, core, T, topo):
     e_win = ev()
     mark(V.tensor_scalar(T.intT[:, 2:4], T.posS[:], 63, None, OP.bitwise_and), e_b)
     mark(V.tensor_scalar(T.intT[:, 4:6], T.posS[:], 0xFC0, None, OP.bitwise_and), e_b)
-    mark(V.tensor_scalar(T.intT[:, 6:8], T.posS[:], 6, 192, OP.logical_shift_right, OP.bitwise_and), e_b)
+    mark(V.tensor_scalar(T.intT[:, 6:8], T.posS[:], 6, 64, OP.logical_shift_right, OP.bitwise_and), e_b)
     wait(V, e_b)
     mark(V.tensor_copy(T.colF[:, 2:8], T.intT[:, 2:8]), e_cf)
     wait(V, e_cf)
     mark(V.tensor_scalar(T.lo64[:], T.colF[:, 2:4], 64.0, None, OP.add), e_l64)
-    mark(V.tensor_scalar(T.a32[:], T.colF[:, 6:8], -32.0, None, OP.add), e_l64)
     wait(V, e_pw0)
     mark(V.tensor_copy(T.win[:, 0:128], T.psW0[:, 0:128]), e_win)
 
@@ -155,18 +155,15 @@ def rank_program(g, core, T, topo):
     wait(V, e_pr)
     for c in range(2):
         mark(V.tensor_reduce(T.rank[:, c:c + 1], T.prod[:, 12 * c:12 * c + 12], AxisListType.X, OP.add), e_rk)
-    wait(V, e_rk, e_ti, e_tix, e_l64)
+    wait(V, e_rk, e_ti, e_tix)
     for B in range(2):
         for c in range(2):
             o = 256 * c + 128 * B
             mark(V.tensor_scalar(T.Einv[:, o:o + 128], T.tabInv[:], 16.0 * B, T.rank[:, c:c + 1],
                                  OP.add, OP.is_equal), e_Ei)
-    for H in range(2):
-        for c in range(2):
-            o = 256 * c + 128 * H
-            acol = T.colF[:, 6 + c:7 + c] if H == 0 else T.a32[:, c:c + 1]
-            mark(V.tensor_scalar(T.Eidx[:, o:o + 128], T.tabIdx[:], acol, T.rank[:, c:c + 1],
-                                 OP.subtract, OP.is_equal), e_Ex)
+    for c in range(2):
+        mark(V.tensor_scalar(T.Eidx[:, 128 * c:128 * c + 128], T.tabIdx[:], T.colF[:, 6 + c:7 + c],
+                             T.rank[:, c:c + 1], OP.subtract, OP.is_equal), e_Ex)
     wait(V, e_pw1)
     mark(V.tensor_copy(T.win[:, 128:256], T.psW1[:, 0:128]), e_win)
 
@@ -177,34 +174,44 @@ def rank_program(g, core, T, topo):
             mark(P.matmul(T.psO[:, 12 * B:12 * B + 12], T.Einv[:, 256 * c + 128 * B:256 * c + 128 * B + 128],
                           T.rhsInv[:, 12 * c:12 * c + 12], c == 0, c == 1), e_po)
     wait(P, e_Ex, e_rx)
-    for H in range(2):
-        i = 0
-        for c in range(2):
-            for rh in (T.rhsHi, T.rhsLo):
-                mark(P.matmul(T.psX[:, 12 * H:12 * H + 12], T.Eidx[:, 256 * c + 128 * H:256 * c + 128 * H + 128],
-                              rh[:, 12 * c:12 * c + 12], i == 0, i == 3), e_px)
-                i += 1
+    i = 0
+    for c in range(2):
+        for rh in (T.rhsHi, T.rhsLo):
+            mark(P.matmul(T.psX[:, 0:12], T.Eidx[:, 128 * c:128 * c + 128],
+                          rh[:, 12 * c:12 * c + 12], i == 0, i == 3), e_px)
+            i += 1
 
-    e_off, e_lown = ev(), ev()
-    e_S = [ev(), ev(), ev()]
-    e_C = [ev(), ev(), ev()]
+    e_off, e_own, e_lown, e_J = ev(), ev(), ev(), ev()
+    e_S = [ev() for _ in range(NS)]
+    e_Z = [ev() for _ in range(NS)]
+
+    def gather(dl, e):
+        mark(V.tensor_copy(T.S[:, MW * dl:MW * dl + 32], T.win[:, 0:256].indirect(T.off[:, 2 * dl:2 * dl + 2])), e)
+
     wait(V, e_po)
     for B in range(2):
         mark(V.tensor_copy(T.off[:, B:24:2], T.psO[:, 12 * B:12 * B + 12]), e_off)
     wait(V, e_off, e_win)
-    for dl in range(1, N):
-        src = T.win[:, 0:256].indirect(T.off[:, 2 * dl:2 * dl + 2])
-        mark(V.tensor_copy(T.S[:, MW * dl:MW * dl + 32], src), e_S[dl // 4])
-        if dl == 3:
-            wait(V, e_px)
-            for H in range(2):
-                mark(V.tensor_copy(T.S[:, MW + 32 + H:N * MW:MW], T.psX[:, 12 * H + 1:12 * H + 12]), e_S[0])
-            mark(V.tensor_copy(T.Cbuf[:, 0:32], T.win[:, 0:256].indirect(T.off[:, 0:2])), e_C[0])
-            mark(V.tensor_copy(T.land[:, L0 + 32:L0 + 34], T.psX[:, 0:24:12]), e_lown)
+    gather(1, e_S[0])
+    wait(V, e_px)
+    mark(V.tensor_copy(T.S[:, MW + 32:N * MW:MW], T.psX[:, 1:12]), e_S[0])
+    gather(2, e_S[1])
+    gather(3, e_S[1])
+    gather(0, e_own)
+    mark(V.tensor_copy(T.ownX[:], T.psX[:, 0:1]), e_lown)
+    wait(V, e_own, e_z)
+    mark(V.tensor_copy(T.Z[0:64, 0:32], T.S[0:64, 0:32]), e_Z[0])
+    wait(A, e_own, e_z)
+    mark(A.activation(T.Z[64:128, 32:64], T.S[64:128, 0:32], COPY), e_Z[0])
+    wait(V, e_id)
+    mark(V.tensor_tensor(T.J[:], T.ident[:, 0:64], T.ident[:, 64:128], OP.add), e_J)
+    for dl in range(4, N):
+        gather(dl, e_S[dl // 2])
 
     sent = 0
-    for c in range(3):
-        dls = [dl for dl in range(4 * c, 4 * c + 4) if dl != 0]
+    arrive = 0
+    for c in range(NS):
+        dls = [dl for dl in (2 * c, 2 * c + 1) if dl != 0]
         dsts = [T.cores[(s - dl) % N] for dl in dls]
         common = topo.mask(core, dsts[0])
         for d in dsts:
@@ -212,74 +219,55 @@ def rank_program(g, core, T, topo):
                 raise ValueError("no direct way")
             common &= topo.mask(core, d)
         eng = [e for e in range(16) if (common >> e) & 1]
-        share = len(eng) // 4
-        sizes = [share] * len(dls)
-        if len(dls) == 3:
-            sizes[0] = 2 * share
+        share = len(eng) // len(dls)
         trs = []
         at = 0
-        for dl, d, n in zip(dls, dsts, sizes):
+        for dl, d in zip(dls, dsts):
             m = 0
-            for e in eng[at:at + n]:
+            for e in eng[at:at + share]:
                 m |= 1 << e
-            at += n
+            at += share
             rid, pid, _se = topo.addr(d)
             trs.append(RemoteDMATransfer(dst_ids=[DstId(rid=rid, pnc=pid)], dma_engine_mask=m,
                                          remote_sem=T.sem["arr%d" % c],
                                          src=T.S[:, MW * dl:MW * dl + MW],
-                                         dst=T.land[:, L0 + MW * dl:L0 + MW * dl + MW]))
-            sent += n
+                                         dst=T.land[:, MW * dl:MW * dl + MW]))
+            sent += share
+        arrive = share * len(dls)
         wait(g, e_S[c])
         g.remote_dma_fused(trs, local_sem=T.sem.sent)
-    arrive = sent // 3
-
-    def scatter(c, H):
-        g.indirect_dma_start(T.y[:], IndirectOffsetOnAxis(ap=T.idxI[:, 2 * c + H:2 * c + H + 1], axis=0),
-                             T.tile[:, 128 * c + 64 * H:128 * c + 64 * H + 64], None,
-                             bounds_check=4095, oob_is_err=False).then_inc(T.sem.scat, 16)
 
     wait(g, e_tab)
     g.wait_ge(T.sem.gtab, 16)
-    for c in range(3):
-        e_r, e_I = ev(), ev()
-        V.wait_ge(T.sem["arr%d" % c], arrive)
-        for q in range(4):
-            dl = 4 * c + q
+    banks = (T.psTa, T.psTb, T.psTc)
+    e_t = [ev() for _ in range(NS)]
+    for t in range(NS):
+        e_I, e_pt = ev(), ev()
+        V.wait_ge(T.sem["arr%d" % t], arrive)
+        A.wait_ge(T.sem["arr%d" % t], arrive)
+        for b in range(2):
+            dl = 2 * t + b
             if dl:
-                mark(V.tensor_copy(T.Cbuf[:, 32 * dl:32 * dl + 32], T.land[:, L0 + MW * dl:L0 + MW * dl + 32]), e_C[c])
-        wait(P, e_C[c])
-        if c == 0:
-            e_pt = [ev(), ev()]
-            for H, ps in enumerate((T.psTa, T.psTb)):
-                mark(P.transpose(ps[:, 0:64], T.Cbuf[64 * H:64 * H + 64, 0:128],
-                                 T.ident[64 * H:64 * H + 64, 64 * H:64 * H + 64]), e_pt[H])
+                o = 128 * t + 64 * b
+                mark(V.tensor_copy(T.Z[0:64, o:o + 32], T.land[0:64, MW * dl:MW * dl + 32]), e_Z[t])
+                mark(A.activation(T.Z[64:128, o + 32:o + 64], T.land[64:128, MW * dl:MW * dl + 32], COPY), e_Z[t])
+        if t == 0:
             wait(V, e_lown)
+            colA = T.ownX[:, 0:1]
         else:
-            e_pt = [ev()]
-            ps = T.psT1 if c == 1 else T.psW0
-            if c == 2:
-                wait(P, e_win)
-            mark(P.transpose(ps[:, 0:128], T.Cbuf[:, 128 * c:128 * c + 128], T.ident[:]), e_pt[0])
-        for H in range(2):
-            a = L0 + 4 * MW * c + 32 + H
-            mark(V.tensor_reduce(T.idxF[:, 2 * c + H:2 * c + H + 1], T.land[:, a:a + 3 * MW + 1:MW],
-                                 AxisListType.X, OP.add), e_r)
-        wait(V, e_r)
-        mark(V.tensor_scalar(T.idxI[:, 2 * c:2 * c + 2], T.idxF[:, 2 * c:2 * c + 2], -64.0, None, OP.add), e_I)
-        wait(g, e_I)
-        if c == 0:
-            for H, ps in enumerate((T.psTa, T.psTb)):
-                e_t = ev()
-                wait(V, e_pt[H])
-                mark(V.tensor_copy(T.tile[:, 64 * H:64 * H + 64], ps[:, 0:64]), e_t)
-                wait(g, e_t)
-                scatter(c, H)
-        else:
-            e_t = ev()
-            wait(V, e_pt[0])
-            mark(V.tensor_copy(T.tile[:, 128 * c:128 * c + 128], ps[:, 0:128]), e_t)
-            wait(g, e_t)
-            scatter(c, 0)
-            scatter(c, 1)
-    g.wait_ge(T.sem.scat, 96)
+            colA = T.land[:, MW * 2 * t + 32:MW * 2 * t + 33]
+        colB = T.land[:, MW * (2 * t + 1) + 32:MW * (2 * t + 1) + 33]
+        mark(V.tensor_scalar(T.idxI[:, t:t + 1], colA, colB, -64.0, OP.add, OP.add), e_I)
+        ps = banks[t % 3]
+        wait(P, e_Z[t], e_z, e_J)
+        if t >= 3:
+            wait(P, e_t[t - 3])
+        mark(P.matmul(ps[:, 0:64], T.Z[:, 128 * t:128 * t + 128], T.J[:], True, True), e_pt)
+        wait(V, e_pt)
+        mark(V.tensor_copy(T.tile[:, 64 * t:64 * t + 64], ps[:, 0:64]), e_t[t])
+        wait(g, e_I, e_t[t])
+        g.indirect_dma_start(T.y[:], IndirectOffsetOnAxis(ap=T.idxI[:, t:t + 1], axis=0),
+                             T.tile[:, 64 * t:64 * t + 64], None,
+                             bounds_check=4095, oob_is_err=False).then_inc(T.sem.scat, 16)
+    g.wait_ge(T.sem.scat, 16 * NS)
     g.wait_ge(T.sem.sent, sent)

@@ -6,48 +6,33 @@ R = 4096
 GROWS = 128
 MW = 33
 NS = 6
+NB = 68
+EARLY = 3
 
 SCRATCH = {
     "posS": ("sbuf", [128, 2], "int32"),
-    "newS": ("sbuf", [128, 256], "float32"),
-    "win": ("sbuf", [128, 256], "float32"),
-    "val": ("sbuf", [128, 2], "float32"),
-    "tabD": ("sbuf", [128, 12], "float32"),
-    "rowi": ("sbuf", [128, 128], "float32"),
-    "ident": ("sbuf", [128, 128], "float32"),
-    "J": ("sbuf", [128, 64], "float32"),
-    "tri": ("sbuf", [128, 128], "bfloat16"),
-    "onesb": ("sbuf", [128, 128], "bfloat16"),
-    "tabInv": ("sbuf", [128, 128], "bfloat16"),
-    "tabIdx": ("sbuf", [128, 128], "bfloat16"),
-    "intT": ("sbuf", [128, 8], "int32"),
-    "colF": ("sbuf", [128, 8], "float32"),
-    "lo64": ("sbuf", [128, 2], "float32"),
-    "D": ("sbuf", [128, 24], "bfloat16"),
-    "rhsInv": ("sbuf", [128, 24], "bfloat16"),
-    "rhsHi": ("sbuf", [128, 24], "bfloat16"),
-    "rhsLo": ("sbuf", [128, 24], "bfloat16"),
-    "prod": ("sbuf", [128, 24], "float32"),
-    "rank": ("sbuf", [128, 2], "float32"),
-    "Einv": ("sbuf", [128, 512], "bfloat16"),
-    "Eidx": ("sbuf", [128, 256], "bfloat16"),
-    "off": ("sbuf", [128, 24], "uint16"),
+    "newS": ("sbuf", [128, 2 * NB], "float32"),
+    "tabD": ("sbuf", [128, N], "float32"),
+    "z": ("sbuf", [128, 128], "float32"),
+    "odd": ("sbuf", [128, 64], "float32"),
+    "w": ("sbuf", [128, 128], "bfloat16"),
+    "dI": ("sbuf", [128, 2], "int32"),
+    "dF": ("sbuf", [128, 2], "float32"),
+    "D": ("sbuf", [128, 2 * N], "bfloat16"),
+    "E": ("sbuf", [128, 128 * 2 * NS], "float32"),
     "S": ("sbuf", [128, N * MW], "float32"),
     "land": ("sbuf", [128, N * MW], "float32"),
-    "ownX": ("sbuf", [128, 1], "float32"),
-    "Z": ("sbuf", [128, 128 * NS], "float32"),
     "tile": ("sbuf", [128, 64 * NS], "float32"),
     "idxI": ("sbuf", [128, NS], "int32"),
-    "psW0": ("psum", [128, 512], "float32"),
-    "psW1": ("psum", [128, 512], "float32"),
-    "psC": ("psum", [128, 512], "float32"),
-    "psO": ("psum", [128, 512], "float32"),
     "psX": ("psum", [128, 512], "float32"),
-    "psTa": ("psum", [128, 512], "float32"),
-    "psTb": ("psum", [128, 512], "float32"),
-    "psTc": ("psum", [128, 512], "float32"),
+    "psB0": ("psum", [128, 512], "float32"),
+    "psB1": ("psum", [128, 512], "float32"),
+    "psB2": ("psum", [128, 512], "float32"),
+    "psB3": ("psum", [128, 512], "float32"),
+    "psB4": ("psum", [128, 512], "float32"),
+    "psB5": ("psum", [128, 512], "float32"),
 }
-NEV = 100
+NEV = 60
 SEMAPHORES = ["arr%d" % i for i in range(NS)] + ["sent", "scat", "gtab"] + ["e%d" % i for i in range(NEV)]
 
 
@@ -76,140 +61,112 @@ def rank_program(g, core, T, topo):
     def iota(out, pattern, base, cm, e):
         mark(g.iota(out, pattern, base, cm, allow_small_or_imprecise_dtypes=True), e)
 
-    e_pos, e_new0, e_new1, e_tab = ev(), ev(), ev(), ev()
+    e_pos, e_tab = ev(), ev()
+    e_new = [ev(), ev()]
     mark(SY.dma_start(T.posS[:], T.pos[:]), e_pos, 16)
-    mark(SY.dma_start(T.newS[:, 0:64], T.new[0:128, :]), e_new0, 16)
-    mark(A.dma_start(T.newS[:, 64:128], T.new[0:128, :]), e_new0, 16)
-    mark(SY.dma_start(T.newS[:, 128:192], T.new[128:256, :]), e_new1, 16)
-    mark(A.dma_start(T.newS[:, 192:256], T.new[128:256, :]), e_new1, 16)
+    mark(SY.dma_start(T.newS[:, 0:64], T.new[0:128, :]), e_new[0], 16)
+    mark(A.dma_start(T.newS[:, NB:NB + 64], T.new[128:256, :]), e_new[1], 16)
     mark(A.dma_start(T.y[0:R - GROWS, :], T.tab[0:R - GROWS, :]), e_tab, 16)
 
-    e_val, e_tabD, e_row, e_ti, e_tix = ev(), ev(), ev(), ev(), ev()
-    iota(T.val[:], [[128, 2]], 0, 1, e_val)
-    iota(T.tabD[:, 0:s + 1], [[-1, s + 1]], s, 0, e_tabD)
-    if s < N - 1:
-        iota(T.tabD[:, s + 1:N], [[-1, N - 1 - s]], N - 1, 0, e_tabD)
-    iota(T.rowi[:], [[1, 128]], 0, 0, e_row)
-    iota(T.tabInv[:], [[32, 2], [0, 4], [1, 16]], 0, 0, e_ti)
-    if s % 2 == 0:
-        iota(T.tabIdx[:], [[64, 2], [1, 64]], 0, 0, e_tix)
-    else:
-        iota(T.tabIdx[:], [[-64, 2], [1, 64]], 64, 0, e_tix)
+    e_z, e_tabD, e_odd = ev(), ev(), ev()
+    iota(T.z[:], [[2, 128]], 1, -2, e_z)
+    iota(T.tabD[:], [[1, N]], 0, 0, e_tabD)
+    iota(T.odd[:], [[2, 64]], 1, 0, e_odd)
     g.dma_start(T.y[R - GROWS:R, :], T.tab[R - GROWS:R, :]).then_inc(T.sem.gtab, 16)
 
-    e_ones, e_id, e_tri, e_z = ev(), ev(), ev(), ev()
-    mark(V.memset(T.onesb[:], 1.0), e_ones)
-    mark(V.memset(T.Z[:, 0:256], 0.0), e_z)
-    wait(A, e_row)
-    for j in range(2, NS):
-        mark(A.activation(T.Z[:, 128 * j:128 * j + 128], T.rowi[:], COPY, scale=0.0), e_z)
-    wait(V, e_val, e_row)
-    mark(V.tensor_scalar(T.tri[:], T.rowi[:], T.val[:, 0:1], None, OP.is_gt), e_tri)
-    mark(V.tensor_scalar(T.ident[:], T.rowi[:], T.val[:, 0:1], None, OP.is_equal), e_id)
+    e_ms, e_w = ev(), ev()
+    mark(V.memset(T.S[:], 0.0), e_ms)
+    wait(V, e_z)
+    mark(V.tensor_scalar(T.w[:], T.z[:], 0.0, 2.0, OP.max, OP.min), e_w)
 
-    e_d, e_df, e_D, e_b, e_cf, e_l64 = ev(), ev(), ev(), ev(), ev(), ev()
+    e_d, e_df, e_D, e_col, e_X = ev(), ev(), ev(), ev(), ev()
     wait(V, e_pos)
-    mark(V.tensor_scalar(T.intT[:, 0:2], T.posS[:], 12, None, OP.arith_shift_right), e_d)
+    mark(V.tensor_scalar(T.dI[:], T.posS[:], 12, None, OP.arith_shift_right), e_d)
     wait(V, e_d)
-    mark(V.tensor_copy(T.colF[:, 0:2], T.intT[:, 0:2]), e_df)
+    mark(V.tensor_copy(T.dF[:], T.dI[:]), e_df)
     wait(V, e_df, e_tabD)
     for c in range(2):
-        mark(V.tensor_scalar(T.D[:, 12 * c:12 * c + 12], T.tabD[:], T.colF[:, c:c + 1], None, OP.is_equal), e_D)
+        mark(V.tensor_scalar(T.D[:, N * c:N * c + N], T.tabD[:], T.dF[:, c:c + 1], None, OP.is_equal), e_D)
+    mark(V.tensor_scalar(T.newS[:, 64:NB + 65:NB], T.posS[:], 1.0, None, OP.add), e_col)
 
-    e_pw0, e_pw1, e_pc = ev(), ev(), ev()
-    wait(P, e_new0, e_id)
-    mark(P.transpose(T.psW0[:, 0:128], T.newS[:, 0:128], T.ident[:]), e_pw0)
-    wait(P, e_D, e_tri, e_ones)
-    mark(P.matmul(T.psC[:, 0:12], T.tri[:], T.D[:, 0:12], True, True), e_pc)
-    mark(P.matmul(T.psC[:, 12:24], T.onesb[:], T.D[:, 0:12], True, False), e_pc)
-    mark(P.matmul(T.psC[:, 12:24], T.tri[:], T.D[:, 12:24], False, True), e_pc)
-    wait(P, e_new1)
-    mark(P.transpose(T.psW1[:, 0:128], T.newS[:, 128:256], T.ident[:]), e_pw1)
+    wait(P, e_w, e_D)
+    mark(P.matmul(T.psX[:, 0:2 * N], T.w[:], T.D[:], True, True), e_X)
 
-    e_win = ev()
-    mark(V.tensor_scalar(T.intT[:, 2:4], T.posS[:], 63, None, OP.bitwise_and), e_b)
-    mark(V.tensor_scalar(T.intT[:, 4:6], T.posS[:], 0xFC0, None, OP.bitwise_and), e_b)
-    mark(V.tensor_scalar(T.intT[:, 6:8], T.posS[:], 6, 64, OP.logical_shift_right, OP.bitwise_and), e_b)
-    wait(V, e_b)
-    mark(V.tensor_copy(T.colF[:, 2:8], T.intT[:, 2:8]), e_cf)
-    wait(V, e_cf)
-    mark(V.tensor_scalar(T.lo64[:], T.colF[:, 2:4], 64.0, None, OP.add), e_l64)
-    wait(V, e_pw0)
-    mark(V.tensor_copy(T.win[:, 0:128], T.psW0[:, 0:128]), e_win)
-
-    e_ri, e_rx = ev(), ev()
-    wait(A, e_D, e_val)
-    for c in range(2):
-        mark(A.activation(T.rhsInv[:, 12 * c:12 * c + 12], T.D[:, 12 * c:12 * c + 12], COPY,
-                          scale=T.val[:, c:c + 1]), e_ri)
-    wait(A, e_cf, e_l64)
-    for c in range(2):
-        mark(A.activation(T.rhsHi[:, 12 * c:12 * c + 12], T.D[:, 12 * c:12 * c + 12], COPY,
-                          scale=T.colF[:, 4 + c:5 + c]), e_rx)
-        mark(A.activation(T.rhsLo[:, 12 * c:12 * c + 12], T.D[:, 12 * c:12 * c + 12], COPY,
-                          scale=T.lo64[:, c:c + 1]), e_rx)
-
-    e_pr, e_rk, e_Ei, e_Ex = ev(), ev(), ev(), ev()
-    wait(V, e_pc, e_D)
-    mark(V.tensor_tensor(T.prod[:], T.psC[:, 0:24], T.D[:], OP.mult), e_pr)
-    wait(V, e_pr)
-    for c in range(2):
-        mark(V.tensor_reduce(T.rank[:, c:c + 1], T.prod[:, 12 * c:12 * c + 12], AxisListType.X, OP.add), e_rk)
-    wait(V, e_rk, e_ti, e_tix)
-    for B in range(2):
-        for c in range(2):
-            o = 256 * c + 128 * B
-            mark(V.tensor_scalar(T.Einv[:, o:o + 128], T.tabInv[:], 16.0 * B, T.rank[:, c:c + 1],
-                                 OP.add, OP.is_equal), e_Ei)
-    for c in range(2):
-        mark(V.tensor_scalar(T.Eidx[:, 128 * c:128 * c + 128], T.tabIdx[:], T.colF[:, 6 + c:7 + c],
-                             T.rank[:, c:c + 1], OP.subtract, OP.is_equal), e_Ex)
-    wait(V, e_pw1)
-    mark(V.tensor_copy(T.win[:, 128:256], T.psW1[:, 0:128]), e_win)
-
-    e_po, e_px = ev(), ev()
-    wait(P, e_Ei, e_ri)
-    for B in range(2):
-        for c in range(2):
-            mark(P.matmul(T.psO[:, 12 * B:12 * B + 12], T.Einv[:, 256 * c + 128 * B:256 * c + 128 * B + 128],
-                          T.rhsInv[:, 12 * c:12 * c + 12], c == 0, c == 1), e_po)
-    wait(P, e_Ex, e_rx)
-    i = 0
-    for c in range(2):
-        for rh in (T.rhsHi, T.rhsLo):
-            mark(P.matmul(T.psX[:, 0:12], T.Eidx[:, 128 * c:128 * c + 128],
-                          rh[:, 12 * c:12 * c + 12], i == 0, i == 3), e_px)
-            i += 1
-
-    e_off, e_own, e_lown, e_J = ev(), ev(), ev(), ev()
+    e_E = [[ev(), ev()] for _ in range(NS)]
+    e_pb = [ev() for _ in range(NS)]
     e_S = [ev() for _ in range(NS)]
-    e_Z = [ev() for _ in range(NS)]
+    e_t = [ev() for _ in range(NS)]
+    banks = [T["psB%d" % t] for t in range(NS)]
 
-    def gather(dl, e):
-        mark(V.tensor_copy(T.S[:, MW * dl:MW * dl + 32], T.win[:, 0:256].indirect(T.off[:, 2 * dl:2 * dl + 2])), e)
+    def places(t):
+        for c in range(2):
+            for b in range(2):
+                d = (s - (2 * t + b)) % N
+                o = 128 * (2 * t + c) + 64 * b
+                col = T.psX[:, N * c + d:N * c + d + 1]
+                if c == 0:
+                    ins = V.tensor_scalar(T.E[:, o:o + 64], T.odd[:], col, None, OP.is_equal)
+                else:
+                    ins = V.tensor_scalar(T.E[:, o:o + 64], T.odd[:], col, 128.0, OP.add, OP.is_equal)
+                mark(ins, e_E[t][c])
 
-    wait(V, e_po)
-    for B in range(2):
-        mark(V.tensor_copy(T.off[:, B:24:2], T.psO[:, 12 * B:12 * B + 12]), e_off)
-    wait(V, e_off, e_win)
-    gather(1, e_S[0])
-    wait(V, e_px)
-    mark(V.tensor_copy(T.S[:, MW + 32:N * MW:MW], T.psX[:, 1:12]), e_S[0])
-    gather(2, e_S[1])
-    gather(3, e_S[1])
-    gather(0, e_own)
-    mark(V.tensor_copy(T.ownX[:], T.psX[:, 0:1]), e_lown)
-    wait(V, e_own, e_z)
-    mark(V.tensor_copy(T.Z[0:64, 0:32], T.S[0:64, 0:32]), e_Z[0])
-    wait(A, e_own, e_z)
-    mark(A.activation(T.Z[64:128, 32:64], T.S[64:128, 0:32], COPY), e_Z[0])
-    wait(V, e_id)
-    mark(V.tensor_tensor(T.J[:], T.ident[:, 0:64], T.ident[:, 64:128], OP.add), e_J)
-    for dl in range(4, N):
-        gather(dl, e_S[dl // 2])
+    def bins(t):
+        for c in range(2):
+            wait(P, e_E[t][c])
+            if t == 0:
+                wait(P, e_new[c], e_col)
+            o = 128 * (2 * t + c)
+            mark(P.matmul(banks[t][:, 0:65], T.E[:, o:o + 128], T.newS[:, NB * c:NB * c + 65], c == 0, c == 1),
+                 e_pb[t])
 
-    sent = 0
-    arrive = 0
+    def message(q, t, b):
+        dl = 2 * t + b
+        ps = banks[t]
+        lo, hi = T.S[0:64, MW * dl:MW * dl + 32], T.S[64:128, MW * dl:MW * dl + 33]
+        if q is V:
+            mark(V.tensor_copy(lo, ps[64 * b:64 * b + 64, 0:32]), e_S[t])
+            mark(V.tensor_copy(hi, ps[64 * b:64 * b + 64, 32:65]), e_S[t])
+        else:
+            mark(A.activation(lo, ps[64 * b:64 * b + 64, 0:32], COPY), e_S[t])
+            mark(A.activation(hi, ps[64 * b:64 * b + 64, 32:65], COPY), e_S[t])
+
+    first = -float(R * s + 1)
+    wait(V, e_X, e_odd)
+    places(0)
+    places(1)
+    bins(0)
+    bins(1)
+    wait(V, e_pb[0], e_ms)
+    message(V, 0, 1)
+    mark(V.tensor_copy(T.tile[0:64, 0:64], banks[0][0:64, 0:64]), e_t[0])
+    mark(V.tensor_scalar(T.idxI[0:64, 0:1], banks[0][0:64, 64:65], first, None, OP.add), e_t[0])
+    for t in range(2, NS):
+        places(t)
+    for t in range(2, NS):
+        bins(t)
+    wait(A, e_ms)
+    for t in range(1, NS):
+        q = V if t == 2 else A
+        wait(q, e_pb[t])
+        message(q, t, 0)
+        message(q, t, 1)
+
+    arrive = [0]
+
+    def receive(t):
+        V.wait_ge(T.sem["arr%d" % t], arrive[0])
+        for b in range(2):
+            dl = 2 * t + b
+            if dl == 0:
+                continue
+            rows = slice(64 * b, 64 * b + 64)
+            mark(V.tensor_copy(T.tile[rows, 64 * t:64 * t + 32], T.land[0:64, MW * dl:MW * dl + 32]), e_t[t])
+            mark(V.tensor_copy(T.tile[rows, 64 * t + 32:64 * t + 64], T.land[64:128, MW * dl:MW * dl + 32]), e_t[t])
+            mark(V.tensor_scalar(T.idxI[rows, t:t + 1], T.land[64:128, MW * dl + 32:MW * dl + 33],
+                                 first, None, OP.add), e_t[t])
+
+    sent = [0]
+    plans = []
     for c in range(NS):
         dls = [dl for dl in (2 * c, 2 * c + 1) if dl != 0]
         dsts = [T.cores[(s - dl) % N] for dl in dls]
@@ -232,42 +189,29 @@ def rank_program(g, core, T, topo):
                                          remote_sem=T.sem["arr%d" % c],
                                          src=T.S[:, MW * dl:MW * dl + MW],
                                          dst=T.land[:, MW * dl:MW * dl + MW]))
-            sent += share
-        arrive = share * len(dls)
-        wait(g, e_S[c])
-        g.remote_dma_fused(trs, local_sem=T.sem.sent)
+            sent[0] += share
+        arrive[0] = share * len(dls)
+        plans.append(trs)
 
+    for t in range(NS):
+        receive(t)
+
+    def call(c):
+        wait(g, e_S[c])
+        g.remote_dma_fused(plans[c], local_sem=T.sem.sent)
+
+    wait(g, e_ms)
+    for c in range(EARLY):
+        call(c)
     wait(g, e_tab)
     g.wait_ge(T.sem.gtab, 16)
-    banks = (T.psTa, T.psTb, T.psTc)
-    e_t = [ev() for _ in range(NS)]
     for t in range(NS):
-        e_I, e_pt = ev(), ev()
-        V.wait_ge(T.sem["arr%d" % t], arrive)
-        A.wait_ge(T.sem["arr%d" % t], arrive)
-        for b in range(2):
-            dl = 2 * t + b
-            if dl:
-                o = 128 * t + 64 * b
-                mark(V.tensor_copy(T.Z[0:64, o:o + 32], T.land[0:64, MW * dl:MW * dl + 32]), e_Z[t])
-                mark(A.activation(T.Z[64:128, o + 32:o + 64], T.land[64:128, MW * dl:MW * dl + 32], COPY), e_Z[t])
-        if t == 0:
-            wait(V, e_lown)
-            colA = T.ownX[:, 0:1]
-        else:
-            colA = T.land[:, MW * 2 * t + 32:MW * 2 * t + 33]
-        colB = T.land[:, MW * (2 * t + 1) + 32:MW * (2 * t + 1) + 33]
-        mark(V.tensor_scalar(T.idxI[:, t:t + 1], colA, colB, -64.0, OP.add, OP.add), e_I)
-        ps = banks[t % 3]
-        wait(P, e_Z[t], e_z, e_J)
-        if t >= 3:
-            wait(P, e_t[t - 3])
-        mark(P.matmul(ps[:, 0:64], T.Z[:, 128 * t:128 * t + 128], T.J[:], True, True), e_pt)
-        wait(V, e_pt)
-        mark(V.tensor_copy(T.tile[:, 64 * t:64 * t + 64], ps[:, 0:64]), e_t[t])
-        wait(g, e_I, e_t[t])
+        wait(g, e_t[t])
         g.indirect_dma_start(T.y[:], IndirectOffsetOnAxis(ap=T.idxI[:, t:t + 1], axis=0),
                              T.tile[:, 64 * t:64 * t + 64], None,
-                             bounds_check=4095, oob_is_err=False).then_inc(T.sem.scat, 16)
+                             bounds_check=R - 1, oob_is_err=False).then_inc(T.sem.scat, 16)
+        if t == 0:
+            for c in range(EARLY, NS):
+                call(c)
     g.wait_ge(T.sem.scat, 16 * NS)
-    g.wait_ge(T.sem.sent, sent)
+    g.wait_ge(T.sem.sent, sent[0])

from concourse.bass import DstId, RemoteDMATransfer, IndirectOffsetOnAxis
from concourse.mybir import AluOpType, AxisListType, ActivationFunctionType

N = 12
R = 4096
GROWS = 128
MW = 33
NS = 6
NB = 68
EARLY = 3

SCRATCH = {
    "posS": ("sbuf", [128, 2], "int32"),
    "newS": ("sbuf", [128, 2 * NB], "float32"),
    "tabD": ("sbuf", [128, N], "float32"),
    "z": ("sbuf", [128, 128], "float32"),
    "odd": ("sbuf", [128, 64], "float32"),
    "w": ("sbuf", [128, 128], "bfloat16"),
    "dI": ("sbuf", [128, 2], "int32"),
    "dF": ("sbuf", [128, 2], "float32"),
    "D": ("sbuf", [128, 2 * N], "bfloat16"),
    "E": ("sbuf", [128, 128 * 2 * NS], "float32"),
    "S": ("sbuf", [128, N * MW], "float32"),
    "land": ("sbuf", [128, N * MW], "float32"),
    "tile": ("sbuf", [128, 64 * NS], "float32"),
    "idxI": ("sbuf", [128, NS], "int32"),
    "psX": ("psum", [128, 512], "float32"),
    "psB0": ("psum", [128, 512], "float32"),
    "psB1": ("psum", [128, 512], "float32"),
    "psB2": ("psum", [128, 512], "float32"),
    "psB3": ("psum", [128, 512], "float32"),
    "psB4": ("psum", [128, 512], "float32"),
    "psB5": ("psum", [128, 512], "float32"),
}
NEV = 60
SEMAPHORES = ["arr%d" % i for i in range(NS)] + ["sent", "scat", "gtab"] + ["e%d" % i for i in range(NEV)]


def rank_program(g, core, T, topo):
    s = T.rank_of(core)
    if s is None:
        return
    V, A, P, SY = g.vector, g.scalar, g.tensor, g.sync
    OP = AluOpType
    COPY = ActivationFunctionType.Copy
    used = [0]

    def ev():
        e = {"s": T.sem["e%d" % used[0]], "n": 0}
        used[0] += 1
        return e

    def mark(ins, e, k=1):
        ins.then_inc(e["s"], k)
        e["n"] += k

    def wait(q, *es):
        for e in es:
            q.wait_ge(e["s"], e["n"])

    def iota(out, pattern, base, cm, e):
        mark(g.iota(out, pattern, base, cm, allow_small_or_imprecise_dtypes=True), e)

    e_pos, e_tab = ev(), ev()
    e_new = [ev(), ev()]
    mark(SY.dma_start(T.posS[:], T.pos[:]), e_pos, 16)
    mark(SY.dma_start(T.newS[:, 0:64], T.new[0:128, :]), e_new[0], 16)
    mark(A.dma_start(T.newS[:, NB:NB + 64], T.new[128:256, :]), e_new[1], 16)
    mark(A.dma_start(T.y[0:R - GROWS, :], T.tab[0:R - GROWS, :]), e_tab, 16)

    e_z, e_tabD, e_odd = ev(), ev(), ev()
    iota(T.z[:], [[2, 128]], 1, -2, e_z)
    iota(T.tabD[:], [[1, N]], 0, 0, e_tabD)
    iota(T.odd[:], [[2, 64]], 1, 0, e_odd)
    g.dma_start(T.y[R - GROWS:R, :], T.tab[R - GROWS:R, :]).then_inc(T.sem.gtab, 16)

    e_ms, e_w = ev(), ev()
    mark(V.memset(T.S[:], 0.0), e_ms)
    wait(V, e_z)
    mark(V.tensor_scalar(T.w[:], T.z[:], 0.0, 2.0, OP.max, OP.min), e_w)

    e_d, e_df, e_D, e_col, e_X = ev(), ev(), ev(), ev(), ev()
    wait(V, e_pos)
    mark(V.tensor_scalar(T.dI[:], T.posS[:], 12, None, OP.arith_shift_right), e_d)
    wait(V, e_d)
    mark(V.tensor_copy(T.dF[:], T.dI[:]), e_df)
    wait(V, e_df, e_tabD)
    for c in range(2):
        mark(V.tensor_scalar(T.D[:, N * c:N * c + N], T.tabD[:], T.dF[:, c:c + 1], None, OP.is_equal), e_D)
    mark(V.tensor_scalar(T.newS[:, 64:NB + 65:NB], T.posS[:], 1.0, None, OP.add), e_col)

    wait(P, e_w, e_D)
    mark(P.matmul(T.psX[:, 0:2 * N], T.w[:], T.D[:], True, True), e_X)

    e_E = [[ev(), ev()] for _ in range(NS)]
    e_pb = [ev() for _ in range(NS)]
    e_S = [ev() for _ in range(NS)]
    e_t = [ev() for _ in range(NS)]
    banks = [T["psB%d" % t] for t in range(NS)]

    def places(t):
        for c in range(2):
            for b in range(2):
                d = (s - (2 * t + b)) % N
                o = 128 * (2 * t + c) + 64 * b
                col = T.psX[:, N * c + d:N * c + d + 1]
                if c == 0:
                    ins = V.tensor_scalar(T.E[:, o:o + 64], T.odd[:], col, None, OP.is_equal)
                else:
                    ins = V.tensor_scalar(T.E[:, o:o + 64], T.odd[:], col, 128.0, OP.add, OP.is_equal)
                mark(ins, e_E[t][c])

    def bins(t):
        for c in range(2):
            wait(P, e_E[t][c])
            if t == 0:
                wait(P, e_new[c], e_col)
            o = 128 * (2 * t + c)
            mark(P.matmul(banks[t][:, 0:65], T.E[:, o:o + 128], T.newS[:, NB * c:NB * c + 65], c == 0, c == 1),
                 e_pb[t])

    def message(q, t, b):
        dl = 2 * t + b
        ps = banks[t]
        lo, hi = T.S[0:64, MW * dl:MW * dl + 32], T.S[64:128, MW * dl:MW * dl + 33]
        if q is V:
            mark(V.tensor_copy(lo, ps[64 * b:64 * b + 64, 0:32]), e_S[t])
            mark(V.tensor_copy(hi, ps[64 * b:64 * b + 64, 32:65]), e_S[t])
        else:
            mark(A.activation(lo, ps[64 * b:64 * b + 64, 0:32], COPY), e_S[t])
            mark(A.activation(hi, ps[64 * b:64 * b + 64, 32:65], COPY), e_S[t])

    first = -float(R * s + 1)
    wait(V, e_X, e_odd)
    places(0)
    places(1)
    bins(0)
    bins(1)
    wait(V, e_pb[0], e_ms)
    message(V, 0, 1)
    mark(V.tensor_copy(T.tile[0:64, 0:64], banks[0][0:64, 0:64]), e_t[0])
    mark(V.tensor_scalar(T.idxI[0:64, 0:1], banks[0][0:64, 64:65], first, None, OP.add), e_t[0])
    for t in range(2, NS):
        places(t)
    for t in range(2, NS):
        bins(t)
    wait(A, e_ms)
    for t in range(1, NS):
        q = V if t == 2 else A
        wait(q, e_pb[t])
        message(q, t, 0)
        message(q, t, 1)

    arrive = [0]

    def receive(t):
        V.wait_ge(T.sem["arr%d" % t], arrive[0])
        for b in range(2):
            dl = 2 * t + b
            if dl == 0:
                continue
            rows = slice(64 * b, 64 * b + 64)
            mark(V.tensor_copy(T.tile[rows, 64 * t:64 * t + 32], T.land[0:64, MW * dl:MW * dl + 32]), e_t[t])
            mark(V.tensor_copy(T.tile[rows, 64 * t + 32:64 * t + 64], T.land[64:128, MW * dl:MW * dl + 32]), e_t[t])
            mark(V.tensor_scalar(T.idxI[rows, t:t + 1], T.land[64:128, MW * dl + 32:MW * dl + 33],
                                 first, None, OP.add), e_t[t])

    sent = [0]
    plans = []
    for c in range(NS):
        dls = [dl for dl in (2 * c, 2 * c + 1) if dl != 0]
        dsts = [T.cores[(s - dl) % N] for dl in dls]
        common = topo.mask(core, dsts[0])
        for d in dsts:
            if not topo.may_write(core, d):
                raise ValueError("no direct way")
            common &= topo.mask(core, d)
        eng = [e for e in range(16) if (common >> e) & 1]
        share = len(eng) // len(dls)
        trs = []
        at = 0
        for dl, d in zip(dls, dsts):
            m = 0
            for e in eng[at:at + share]:
                m |= 1 << e
            at += share
            rid, pid, _se = topo.addr(d)
            trs.append(RemoteDMATransfer(dst_ids=[DstId(rid=rid, pnc=pid)], dma_engine_mask=m,
                                         remote_sem=T.sem["arr%d" % c],
                                         src=T.S[:, MW * dl:MW * dl + MW],
                                         dst=T.land[:, MW * dl:MW * dl + MW]))
            sent[0] += share
        arrive[0] = share * len(dls)
        plans.append(trs)

    for t in range(NS):
        receive(t)

    def call(c):
        wait(g, e_S[c])
        g.remote_dma_fused(plans[c], local_sem=T.sem.sent)

    wait(g, e_ms)
    for c in range(EARLY):
        call(c)
    wait(g, e_tab)
    g.wait_ge(T.sem.gtab, 16)
    for t in range(NS):
        wait(g, e_t[t])
        g.indirect_dma_start(T.y[:], IndirectOffsetOnAxis(ap=T.idxI[:, t:t + 1], axis=0),
                             T.tile[:, 64 * t:64 * t + 64], None,
                             bounds_check=R - 1, oob_is_err=False).then_inc(T.sem.scat, 16)
        if t == 0:
            for c in range(EARLY, NS):
                call(c)
    g.wait_ge(T.sem.scat, 16 * NS)
    g.wait_ge(T.sem.sent, sent[0])
